import numpy as np
CORES = [7,15,23,31,39,47,55,63,71,79]
N = 10
ROOT = 9
def setup_inputs(rng):
    return {"x": rng.standard_normal((N, 128, 128), dtype=np.float32)}
def reference(x):
    return {"y": np.broadcast_to(x[ROOT], x.shape)}

@@ -1,0 +1,49 @@
+from concourse.bass import DstId, RemoteDMATransfer
+
+SCRATCH = {
+    "land": ("sbuf", [128, 128], "float32"),
+}
+SEMAPHORES = ["loaded", "arrived", "sent", "stored"]
+
+OFF_CHIP = 0x00FF
+NENG = 8
+
+
+def _send(g, T, topo, dsts):
+    ids = []
+    for d in dsts:
+        rid, pid, _se = topo.addr(d)
+        ids.append(DstId(rid=rid, pnc=pid))
+    g.remote_dma_fused(
+        [RemoteDMATransfer(dst_ids=ids, dma_engine_mask=OFF_CHIP, remote_sem=T.sem.arrived,
+                           srcs=[T.land[:]], dsts=[T.land[:] for _d in dsts])],
+        local_sem=T.sem.sent)
+
+
+def rank_program(g, core, T, topo):
+    rank = T.rank_of(core)
+    if rank is None:
+        return
+    root = T.cores[T.root]
+    rchip = topo.chip(root)
+    others = [c for c in T.cores if c != root]
+    plane = [c for c in others if topo.same_plane(topo.chip(c), rchip)]
+    relay = [c for c in others if topo.mates(topo.chip(c), rchip)][0]
+    far = [c for c in others if c != relay and c not in plane]
+
+    if core == root:
+        g.sync.dma_start(T.y[:], T.x[:]).then_inc(T.sem.stored, 16)
+        g.dma_start(T.land[:], T.x[:]).then_inc(T.sem.loaded, 16)
+        g.wait_ge(T.sem.loaded, 16)
+        _send(g, T, topo, [relay] + plane)
+        g.wait_ge(T.sem.sent, NENG)
+        g.wait_ge(T.sem.stored, 16)
+        return
+
+    g.sync.wait_ge(T.sem.arrived, NENG)
+    g.sync.dma_start(T.y[:], T.land[:]).then_inc(T.sem.stored, 16)
+    if core == relay:
+        g.wait_ge(T.sem.arrived, NENG)
+        _send(g, T, topo, far)
+        g.wait_ge(T.sem.sent, NENG)
+    g.wait_ge(T.sem.stored, 16)

@@ -1,49 +1,55 @@
 from concourse.bass import DstId, RemoteDMATransfer
 
+NPIECE = 16
 SCRATCH = {
-    "land": ("sbuf", [128, 128], "float32"),
+    "blk": ("dram", [NPIECE, 128, 8], "float32"),
 }
-SEMAPHORES = ["loaded", "arrived", "sent", "stored"]
-
-OFF_CHIP = 0x00FF
-NENG = 8
+SEMAPHORES = ["loaded", "got", "arrived", "sent", "stored"]
 
 
-def _send(g, T, topo, dsts):
-    ids = []
-    for d in dsts:
-        rid, pid, _se = topo.addr(d)
-        ids.append(DstId(rid=rid, pnc=pid))
-    g.remote_dma_fused(
-        [RemoteDMATransfer(dst_ids=ids, dma_engine_mask=OFF_CHIP, remote_sem=T.sem.arrived,
-                           srcs=[T.land[:]], dsts=[T.land[:] for _d in dsts])],
-        local_sem=T.sem.sent)
+def _write_pieces(g, T, topo, core, jobs, remote_sem):
+    off, on = 0, 8
+    transfers = []
+    for t, dst in jobs:
+        if topo.chip(dst) == topo.chip(core):
+            eng, on = on, on + 1
+        else:
+            eng, off = off, off + 1
+        rid, pid, _se = topo.addr(dst)
+        transfers.append(RemoteDMATransfer(dst_ids=[DstId(rid=rid, pnc=pid)], dma_engine_mask=1 << eng,
+                                           remote_sem=remote_sem, src=T.blk[t], dst=T.blk[t]))
+    g.remote_dma_fused(transfers, local_sem=T.sem.sent)
+    return len(jobs)
 
 
 def rank_program(g, core, T, topo):
-    rank = T.rank_of(core)
-    if rank is None:
-        return
     root = T.cores[T.root]
-    rchip = topo.chip(root)
-    others = [c for c in T.cores if c != root]
-    plane = [c for c in others if topo.same_plane(topo.chip(c), rchip)]
-    relay = [c for c in others if topo.mates(topo.chip(c), rchip)][0]
-    far = [c for c in others if c != relay and c not in plane]
+    takers = [c for c in T.cores if c != root]
+    carriers = []
+    for c in takers:
+        if not topo.mates(topo.chip(c), topo.chip(root)):
+            carriers += [c, c - 4]
 
     if core == root:
-        g.sync.dma_start(T.y[:], T.x[:]).then_inc(T.sem.stored, 16)
-        g.dma_start(T.land[:], T.x[:]).then_inc(T.sem.loaded, 16)
+        g.scalar.dma_start(T.y[:], T.x[:]).then_inc(T.sem.stored, 16)
+        g.sync.dma_start(T.blk[:], T.x[:]).then_inc(T.sem.loaded, 16)
         g.wait_ge(T.sem.loaded, 16)
-        _send(g, T, topo, [relay] + plane)
-        g.wait_ge(T.sem.sent, NENG)
+        n = 0
+        for d in (0, 1):
+            n += _write_pieces(g, T, topo, core, [(t, carriers[t]) for t in range(d, NPIECE, 2)], T.sem.got)
+        g.wait_ge(T.sem.sent, n)
         g.wait_ge(T.sem.stored, 16)
         return
 
-    g.sync.wait_ge(T.sem.arrived, NENG)
-    g.sync.dma_start(T.y[:], T.land[:]).then_inc(T.sem.stored, 16)
-    if core == relay:
-        g.wait_ge(T.sem.arrived, NENG)
-        _send(g, T, topo, far)
-        g.wait_ge(T.sem.sent, NENG)
-    g.wait_ge(T.sem.stored, 16)
+    mine = carriers.index(core) if core in carriers else None
+    if mine is not None:
+        g.wait_ge(T.sem.got, 1)
+        n = _write_pieces(g, T, topo, core, [(mine, c) for c in takers if c != core], T.sem.arrived)
+        g.wait_ge(T.sem.sent, n)
+
+    if core in takers:
+        if mine is not None:
+            g.sync.wait_ge(T.sem.got, 1)
+        g.sync.wait_ge(T.sem.arrived, NPIECE - (0 if mine is None else 1))
+        g.sync.dma_start(T.y[:], T.blk[:]).then_inc(T.sem.stored, 16)
+        g.wait_ge(T.sem.stored, 16)

from concourse.bass import DstId, RemoteDMATransfer

NPIECE = 16
SCRATCH = {
    "blk": ("dram", [NPIECE, 128, 8], "float32"),
}
SEMAPHORES = ["loaded", "got", "arrived", "sent", "stored"]


def _write_pieces(g, T, topo, core, jobs, remote_sem):
    off, on = 0, 8
    transfers = []
    for t, dst in jobs:
        if topo.chip(dst) == topo.chip(core):
            eng, on = on, on + 1
        else:
            eng, off = off, off + 1
        rid, pid, _se = topo.addr(dst)
        transfers.append(RemoteDMATransfer(dst_ids=[DstId(rid=rid, pnc=pid)], dma_engine_mask=1 << eng,
                                           remote_sem=remote_sem, src=T.blk[t], dst=T.blk[t]))
    g.remote_dma_fused(transfers, local_sem=T.sem.sent)
    return len(jobs)


def rank_program(g, core, T, topo):
    root = T.cores[T.root]
    takers = [c for c in T.cores if c != root]
    carriers = []
    for c in takers:
        if not topo.mates(topo.chip(c), topo.chip(root)):
            carriers += [c, c - 4]

    if core == root:
        g.scalar.dma_start(T.y[:], T.x[:]).then_inc(T.sem.stored, 16)
        g.sync.dma_start(T.blk[:], T.x[:]).then_inc(T.sem.loaded, 16)
        g.wait_ge(T.sem.loaded, 16)
        n = 0
        for d in (0, 1):
            n += _write_pieces(g, T, topo, core, [(t, carriers[t]) for t in range(d, NPIECE, 2)], T.sem.got)
        g.wait_ge(T.sem.sent, n)
        g.wait_ge(T.sem.stored, 16)
        return

    mine = carriers.index(core) if core in carriers else None
    if mine is not None:
        g.wait_ge(T.sem.got, 1)
        n = _write_pieces(g, T, topo, core, [(mine, c) for c in takers if c != core], T.sem.arrived)
        g.wait_ge(T.sem.sent, n)

    if core in takers:
        if mine is not None:
            g.sync.wait_ge(T.sem.got, 1)
        g.sync.wait_ge(T.sem.arrived, NPIECE - (0 if mine is None else 1))
        g.sync.dma_start(T.y[:], T.blk[:]).then_inc(T.sem.stored, 16)
        g.wait_ge(T.sem.stored, 16)
